import numpy as np
import ml_dtypes


def mxq(x, axis, fmt="e4m3"):
    dtype, down = {"e4m3": (ml_dtypes.float8_e4m3fn, 7), "e5m2": (ml_dtypes.float8_e5m2, 14)}[fmt]
    v = np.moveaxis(np.asarray(x, np.float32).astype(ml_dtypes.bfloat16).astype(np.float64), axis, -1)
    blocks = v.reshape(v.shape[:-1] + (-1, 32))
    amax = np.abs(blocks).max(-1, keepdims=True)
    byte = np.maximum(np.where(amax > 0, np.frexp(amax)[1] - 1 + 127, 0) - down, 1)
    scale = np.exp2(byte - 127.0)
    codes = (blocks / scale).astype(np.float32).astype(dtype).astype(np.float64)
    return np.moveaxis((codes * scale).reshape(v.shape), -1, axis)


WIDE = False


def mx_kscale(k):
    if not WIDE:
        return np.ones(k)
    levels = np.array([10, -10, 5, -5, 0])
    if k % 512:
        return np.exp2(np.random.permutation(np.resize(levels, k // 32))).repeat(32)
    a = np.empty((k // 512, 16))
    for p in range(k // 512):
        a[p, :8] = np.random.permutation(np.resize(levels, 8))
        for g in range(8):
            far = levels[np.abs(levels - a[p, g]) >= 10]
            a[p, g + 8] = far[np.random.randint(len(far))]
    return np.exp2(a.ravel()).repeat(32)


BF16 = ml_dtypes.bfloat16


def bf(x):
    return np.asarray(x, np.float32).astype(BF16)


def f64(x):
    return np.asarray(x).astype(np.float64)


E2M1 = np.array([0.0, 0.5, 1.0, 1.5, 2.0, 3.0, 4.0, 6.0, -0.0, -0.5, -1.0, -1.5, -2.0, -3.0, -4.0, -6.0])


def pack_weight(w, fmt):
    k, n = w.shape
    w = f64(bf(w)).reshape(k // 32, 32, n)
    amax = np.abs(w).max(1)
    if fmt == "e4m3":
        byte = np.frexp(amax)[1] - 1 + 127 - 7
    else:
        mant, ex = np.frexp(amax / 6.0)
        byte = np.where(mant > 0.5, ex, ex - 1) + 127
    byte = np.clip(np.where(amax > 0, byte, 1), 1, 254)
    scaled = (w * np.exp2(127.0 - byte)[:, None, :]).reshape(k, n).astype(np.float32)
    by_word = np.ascontiguousarray(scaled.reshape(k // 512, 128, 4, n).transpose(0, 1, 3, 2))
    if fmt == "e4m3":
        words = by_word.astype(ml_dtypes.float8_e4m3fn).view(np.uint8)
    else:
        c = by_word.astype(ml_dtypes.float4_e2m1fn).view(np.uint8) & 0xF
        words = c[..., 0::2] | (c[..., 1::2] << 4)
    return np.ascontiguousarray(words), np.ascontiguousarray(byte.astype(np.uint8).reshape(k // 512, 16, n))


def unpack_weight(words, scales, fmt):
    g, p, n, _ = words.shape
    if fmt == "e4m3":
        vals = np.ascontiguousarray(words).view(ml_dtypes.float8_e4m3fn).astype(np.float64)
    else:
        nib = np.empty((g, p, n, 4), np.uint8)
        nib[..., 0::2] = words & 0xF
        nib[..., 1::2] = words >> 4
        vals = E2M1[nib]
    vals = vals * np.repeat(np.exp2(scales.astype(np.float64) - 127.0), 8, axis=1)[..., None]
    return vals.transpose(0, 1, 3, 2).reshape(g * 512, n)
def pack4(w):
    words, scales = pack_weight(w, "e2m1")
    return words.reshape(words.shape[0], 128, -1), scales


def unpack4(words, scales):
    return unpack_weight(words.reshape(words.shape[0], 128, -1, 2), scales, "e2m1")


E4M3FN = np.array([(-1.0 if i & 128 else 1.0) * ((1.0 + (i & 7) / 8.0) * 2.0 ** (((i >> 3) & 15) - 7) if i & 120 else (i & 7) * 2.0 ** -9) for i in range(256)])


def e4m3fn_bytes(y):
    return np.clip(np.asarray(y, np.float64), -448.0, 448.0).astype(np.float32).astype(ml_dtypes.float8_e4m3fn).view(np.uint8)


def e4m3fn_values(b):
    return E4M3FN[b]


B, P, S, K, C = 2, 1024, 512, 1024, 512


def instance_norm(x):
    mu = np.mean(x, axis=1, keepdims=True)
    centered = x - mu
    var = np.mean(centered * centered, axis=1, keepdims=True)
    return centered / np.sqrt(var + 1e-5)


def draw0():
    s, t = mx_kscale(S), mx_kscale(K)
    x = bf(0.5 + 1.5 * np.random.standard_normal((B, P, C)))
    m = bf(np.random.standard_normal((B, P, S)) * s)
    wm_words, wm_scales = pack4(np.random.standard_normal((S, K)) / np.sqrt(S) / s[:, None])
    bm = bf(0.3 * np.random.standard_normal(K))
    g = bf(np.random.standard_normal(K) * t)
    wg_words, wg_scales = pack4(np.random.standard_normal((K, C)) / np.sqrt(K) / t[:, None])
    wb_words, wb_scales = pack4(np.random.standard_normal((K, C)) / np.sqrt(K) / t[:, None])
    return {
        "x": x,
        "m": m,
        "wm_words": wm_words,
        "wm_scales": wm_scales,
        "bm": bm,
        "g": g,
        "wg_words": wg_words,
        "wg_scales": wg_scales,
        "wb_words": wb_words,
        "wb_scales": wb_scales,
    }


def core(x, m, wm_words, wm_scales, bm, g, wg_words, wg_scales, wb_words, wb_scales):
    h = (mxq(f64(m), 2, "e4m3") @ unpack4(wm_words, wm_scales)) + f64(bm)[None, None, :]
    a = np.maximum(h, 0.0) * f64(g)[None, None, :]
    aq = mxq(a, 2, "e4m3")
    gamma = aq @ unpack4(wg_words, wg_scales)
    beta = aq @ unpack4(wb_words, wb_scales)
    xn = instance_norm(f64(x))
    y = xn * (1.0 + gamma) + beta
    return np.where(y >= 0.0, y, 0.2 * y)


def setup_inputs():
    drawn = draw0()
    full = np.asarray(drawn['m']).astype(np.float64)
    scale = (np.abs(full).reshape(2, 8, 128, 4, 128).max(axis=(2, 4)) / 448.0).astype(np.float32)
    given = {}
    for key, value in drawn.items():
        if key == 'm':
            given['m_bytes'] = e4m3fn_bytes(full / np.repeat(np.repeat(scale.astype(np.float64), 128, axis=1), 128, axis=2))
            given['m_scale'] = scale
        else:
            given[key] = value
    return given


def reference(x, m_bytes, m_scale, wm_words, wm_scales, bm, g, wg_words, wg_scales, wb_words, wb_scales):
    return core(x, e4m3fn_values(m_bytes) * np.repeat(np.repeat(m_scale.astype(np.float64), 128, axis=1), 128, axis=2), wm_words, wm_scales, bm, g, wg_words, wg_scales, wb_words, wb_scales)

@@ -1,0 +1,319 @@
+from contextlib import ExitStack
+
+import concourse.mybir as mybir
+from concourse.masks import make_identity
+
+F32 = mybir.dt.float32
+BF16 = mybir.dt.bfloat16
+U32 = mybir.dt.uint32
+I32 = mybir.dt.int32
+U8 = mybir.dt.uint8
+FP8 = mybir.dt.float8_e4m3fn
+FP8X4 = mybir.dt.float8_e4m3fn_x4
+FP4X4 = mybir.dt.float4_e2m1fn_x4
+ALU = mybir.AluOpType
+ACT = mybir.ActivationFunctionType
+
+FLOPS = 2 * 2048 * 512 * 1024 + 2 * 2 * 2048 * 1024 * 512
+
+P = 128
+S = 512
+K = 1024
+C = 512
+R = 4
+CHUNKS = 4
+NT = P * R
+EPS = 1e-5
+VECTOR_INTERLEAVES = ((0, None, 0), (3, 1, 1))
+
+
+def tile_spademodulationpointwise_d2p_kernel(
+    tc, x, m_bytes, m_scale, wm_words, wm_scales, bm, g, wg_words, wg_scales, wb_words, wb_scales, out
+):
+    nc = tc.nc
+    m_view = m_bytes.rearrange("a (h p r) k -> a h p r k", h=2, p=P, r=R)
+    x_view = x.rearrange("a (h p r) c -> a h p r c", h=2, p=P, r=R)
+    out_view = out.rearrange("a (h p r) c -> a h p r c", h=2, p=P, r=R)
+
+    with ExitStack() as ctx:
+        keep = ctx.enter_context(tc.tile_pool(name="keep", bufs=1))
+        work = ctx.enter_context(tc.tile_pool(name="work", bufs=2))
+        psum = ctx.enter_context(tc.psum_pool(name="psum", bufs=1))
+
+        ms_all = keep.tile([P, 64], F32, name="ms_all")
+        nc.scalar.dma_start(out=ms_all[:], in_=m_scale.rearrange("a i j -> (a i j)").partition_broadcast(P))
+        m_raw = [keep.tile([P, R, S], U8, name=f"m_raw{c}", align_bytes=64) for c in range(CHUNKS)]
+        x_sb = [keep.tile([P, R, C], BF16, name=f"x_sb{c}", align_bytes=64) for c in range(CHUNKS)]
+
+        def load_m(c):
+            nc.sync.dma_start(out=m_raw[c][:], in_=m_view[c // 2, c % 2])
+
+        def load_x(c):
+            nc.sync.dma_start(out=x_sb[c][:], in_=x_view[c // 2, c % 2])
+
+        wm_raw = keep.tile([P, 2 * K], U8, name="wm_raw", align_bytes=64)
+        wms_raw = keep.tile([P, K], U8, name="wms_raw", align_bytes=64)
+        wg_sb = keep.tile([P, 2, 2 * C], U8, name="wg_sb", align_bytes=64)
+        wb_sb = keep.tile([P, 2, 2 * C], U8, name="wb_sb", align_bytes=64)
+        wgs = keep.tile([P, 2, C], U8, name="wgs", align_bytes=64)
+        wbs = keep.tile([P, 2, C], U8, name="wbs", align_bytes=64)
+        g_bf = keep.tile([P, 2, 4], BF16, name="g_bf")
+        bm_bf = keep.tile([P, 2, 4], BF16, name="bm_bf")
+
+        nc.gpsimd.memset(wms_raw[:].bitcast(I32), 0)
+        nc.gpsimd.memset(wgs[:].rearrange("p g n -> p (g n)").bitcast(I32), 0)
+        nc.gpsimd.memset(wbs[:].rearrange("p g n -> p (g n)").bitcast(I32), 0)
+
+        load_m(0)
+        nc.sync.dma_start(out=wm_raw[:], in_=wm_words[0])
+        for q in range(4):
+            nc.sync.dma_start(
+                out=wms_raw[32 * q : 32 * q + 4, :].bitcast(I32), in_=wm_scales[0, 4 * q : 4 * q + 4, :].bitcast(I32)
+            )
+        nc.scalar.dma_start(out=g_bf[:], in_=g.rearrange("(g p t) -> p g t", p=P, t=4))
+        nc.scalar.dma_start(out=bm_bf[:], in_=bm.rearrange("(g p t) -> p g t", p=P, t=4))
+        load_x(0)
+        load_x(1)
+        load_m(1)
+        for q in range(4):
+            nc.sync.dma_start(
+                out=wgs[32 * q : 32 * q + 4].bitcast(I32),
+                in_=wg_scales[:, 4 * q : 4 * q + 4, :].rearrange("g q n -> q g n").bitcast(I32),
+            )
+            nc.sync.dma_start(
+                out=wbs[32 * q : 32 * q + 4].bitcast(I32),
+                in_=wb_scales[:, 4 * q : 4 * q + 4, :].rearrange("g q n -> q g n").bitcast(I32),
+            )
+        nc.sync.dma_start(out=wg_sb[:], in_=wg_words.rearrange("g p n -> p g n"))
+        nc.sync.dma_start(out=wb_sb[:], in_=wb_words.rearrange("g p n -> p g n"))
+        load_m(2)
+        load_m(3)
+        load_x(2)
+        load_x(3)
+
+        ident = keep.tile([P, P], F32, name="ident")
+        make_identity(nc, ident[:])
+        ones_bf = keep.tile([P, P], BF16, name="ones_bf")
+        nc.gpsimd.memset(ones_bf[:], 1.0)
+        ones_f = keep.tile([P, P], F32, name="ones_f")
+        nc.gpsimd.memset(ones_f[:], 1.0)
+
+        sc = keep.tile([P, CHUNKS, 4], F32, name="sc")
+        ms_q = ms_all[:].rearrange("p (c q j) -> p c q j", q=4, j=4)
+        for q in range(4):
+            rows = slice(32 * q, 32 * q + 32)
+            nc.gpsimd.tensor_copy(out=sc[rows], in_=ms_q[rows, :, q, :])
+
+        sg = keep.tile([P, 8], F32, name="sg")
+        ga = keep.tile([P, 8], F32, name="ga")
+        gb = keep.tile([P, 8], F32, name="gb")
+        g_flat = g_bf[:].rearrange("p g t -> p (g t)")
+        nc.vector.tensor_scalar(out=sg[:], in0=g_flat, scalar1=0.0, scalar2=2.0, op0=ALU.is_ge, op1=ALU.mult)
+        nc.vector.tensor_scalar(out=sg[:], in0=sg[:], scalar1=-1.0, scalar2=None, op0=ALU.add)
+        nc.vector.tensor_tensor(out=ga[:], in0=g_flat, in1=sg[:], op=ALU.mult)
+        nc.vector.tensor_tensor(out=gb[:], in0=bm_bf[:].rearrange("p g t -> p (g t)"), in1=ga[:], op=ALU.mult)
+
+        m_codes = [keep.tile([P, NT], U32, name=f"m_codes{c}", align_bytes=64) for c in range(CHUNKS)]
+        m_scl = [keep.tile([P, NT], U8, name=f"m_scl{c}", align_bytes=64) for c in range(CHUNKS)]
+
+        def prep(c):
+            m_bf = work.tile([P, R, S], BF16, name="m_bf", align_bytes=64)
+            m_gr = work.tile([P, R * S], BF16, name="m_gr", align_bytes=64)
+            for half in range(2):
+                rs = slice(2 * half, 2 * half + 2)
+                nc.scalar.copy(
+                    out=m_bf[:, rs, :].rearrange("p r k -> p (r k)"),
+                    in_=m_raw[c][:, rs, :].rearrange("p r k -> p (r k)").bitcast(FP8),
+                )
+            for j in range(4):
+                ks = slice(128 * j, 128 * j + 128)
+                nc.vector.tensor_scalar(
+                    out=m_bf[:, :, ks],
+                    in0=m_bf[:, :, ks],
+                    scalar1=sc[:, c, j : j + 1],
+                    scalar2=None,
+                    op0=ALU.mult,
+                )
+            for half in range(2):
+                tp = psum.tile([P, 2, 2, P], F32, name="tp", bufs=1)
+                for r2 in range(2):
+                    words = m_bf[:, 2 * half + r2, :].bitcast(F32)
+                    for u in range(2):
+                        nc.tensor.transpose(tp[:, r2, u, :], words[:, u : 256 : 2], ident[:])
+                nc.scalar.copy(
+                    out=m_gr[:, 1024 * half : 1024 * half + 1024].bitcast(F32).rearrange("p (r t u) -> p r t u", r=2, u=2),
+                    in_=tp[:].rearrange("p r u t -> p r t u"),
+                )
+            nc.vector.quantize_mx(out=m_codes[c][:].bitcast(FP8X4), scales=m_scl[c][:], in_=m_gr[:])
+
+        wm_perm = keep.tile([P, 2, 4, 256], U8, name="wm_perm", align_bytes=64)
+        wms_perm = keep.tile([P, 2, 4, P], U8, name="wms_perm", align_bytes=64)
+
+        def permute_wm():
+            for gg in range(2):
+                nc.vector.tensor_copy(
+                    out=wm_perm[:, gg].rearrange("p t (m b) -> p t m b", b=2),
+                    in_=wm_raw[:, 1024 * gg : 1024 * gg + 1024].rearrange("p (m t b) -> p t m b", t=4, b=2),
+                )
+                nc.vector.tensor_copy(
+                    out=wms_perm[:, gg], in_=wms_raw[:, 512 * gg : 512 * gg + 512].rearrange("p (m t) -> p t m", t=4)
+                )
+
+        nmu = [keep.tile([P, C], F32, name=f"nmu{a}") for a in range(2)]
+        rstd = [keep.tile([P, C], F32, name=f"rstd{a}") for a in range(2)]
+
+        def stats(a):
+            tiles = [x_sb[2 * a + h][:, r, :] for h in range(2) for r in range(R)]
+            s1 = psum.tile([P, C], F32, name="gb_ps", bufs=4)
+            for i, t in enumerate(tiles):
+                nc.tensor.matmul(s1[:], lhsT=ones_bf[:], rhs=t, start=(i == 0), stop=(i == 7))
+            gram = psum.tile([P, 4, P], F32, name="gb_ps", bufs=4)
+            for b in range(4):
+                cols = slice(128 * b, 128 * b + 128)
+                for i, t in enumerate(tiles):
+                    nc.tensor.matmul(gram[:, b, :], lhsT=t[:, cols], rhs=t[:, cols], start=(i == 0), stop=(i == 7))
+            diag = work.tile([P, 4, P], F32, name="diag")
+            nc.vector.tensor_tensor(
+                out=diag[:], in0=gram[:], in1=ident[:].unsqueeze(1).to_broadcast([P, 4, P]), op=ALU.mult
+            )
+            s2 = psum.tile([P, C], F32, name="gb_ps", bufs=4)
+            nc.tensor.matmul(s2[:], lhsT=ones_f[:], rhs=diag[:].rearrange("p b c -> p (b c)"), start=True, stop=True)
+            musq = work.tile([P, C], F32, name="musq")
+            nc.scalar.activation(out=nmu[a][:], in_=s1[:], func=ACT.Copy, scale=-1.0 / 1024.0)
+            nc.scalar.activation(out=musq[:], in_=s1[:], func=ACT.Square, scale=1.0 / 1024.0)
+            var = work.tile([P, C], F32, name="var")
+            nc.vector.scalar_tensor_tensor(
+                out=var[:], in0=s2[:], scalar=1.0 / 1024.0, in1=musq[:], op0=ALU.mult, op1=ALU.subtract
+            )
+            nc.scalar.activation(out=rstd[a][:], in_=var[:], func=ACT.Abs_reciprocal_sqrt, bias=EPS)
+
+        xn = {}
+
+        def normalise(c, engine, half):
+            a = c // 2
+            rs = slice(2 * half, 2 * half + 2)
+            t = work.tile([P, 2, C], F32, name=f"xn{half}", bufs=1 + half)
+            engine.tensor_tensor(
+                out=t[:], in0=x_sb[c][:, rs, :], in1=nmu[a][:].unsqueeze(1).to_broadcast([P, 2, C]), op=ALU.add
+            )
+            engine.tensor_tensor(
+                out=t[:], in0=t[:], in1=rstd[a][:].unsqueeze(1).to_broadcast([P, 2, C]), op=ALU.mult
+            )
+            xn[c, half] = t
+
+        a_codes = {}
+        a_scl = {}
+
+        def stage1(c, half=None):
+            lo, n = (0, NT) if half is None else (half * NT // 2, NT // 2)
+            for gg in range(2):
+                yb = work.tile([P, 4, n], BF16, name="yb", align_bytes=64)
+                for t in range(4):
+                    h = psum.tile([P, n], F32, name="h_ps", bufs=3)
+                    nc.tensor.matmul_mx(
+                        out=h[:],
+                        lhsT=wm_perm[:, gg, t, :].bitcast(FP4X4),
+                        lhsT_scale=wms_perm[:, gg, t, :],
+                        rhs=m_codes[c][:, lo : lo + n].bitcast(FP8X4),
+                        rhs_scale=m_scl[c][:, lo : lo + n],
+                        start=True,
+                        stop=True,
+                    )
+                    col = 4 * gg + t
+                    nc.scalar.activation(
+                        out=yb[:, t, :],
+                        in_=h[:],
+                        func=ACT.Relu,
+                        bias=gb[:, col : col + 1],
+                        scale=ga[:, col : col + 1],
+                    )
+                    nc.vector.tensor_scalar(
+                        out=yb[:, t, :], in0=yb[:, t, :], scalar1=sg[:, col : col + 1], scalar2=None, op0=ALU.mult
+                    )
+                ag = work.tile([P, n, 4], BF16, name="ag", align_bytes=64)
+                ysrc = yb[:].rearrange("p t n -> p n t")
+                if (c, half, gg) in VECTOR_INTERLEAVES:
+                    nc.vector.tensor_copy(out=ag[:], in_=ysrc)
+                else:
+                    nc.scalar.copy(out=ag[:], in_=ysrc)
+                codes = work.tile([P, n], U32, name=f"a_codes{gg}", align_bytes=64)
+                scl = work.tile([P, n], U8, name=f"a_scl{gg}", align_bytes=64)
+                nc.vector.quantize_mx(out=codes[:].bitcast(FP8X4), scales=scl[:], in_=ag[:].rearrange("p n t -> p (n t)"))
+                for r in range(lo // P, (lo + n) // P):
+                    toks = slice(P * r - lo, P * r - lo + P)
+                    a_codes[c, r, gg] = codes[:, toks]
+                    a_scl[c, r, gg] = scl[:, toks]
+
+        y_tiles = {}
+
+        def stage2(c, half):
+            if half == 0:
+                y_tiles[c] = work.tile([P, R, C], F32, name="y")
+            y = y_tiles[c]
+
+            def leaky(rs):
+                nc.vector.scalar_tensor_tensor(
+                    out=y[:, rs, :], in0=y[:, rs, :], scalar=0.2, in1=y[:, rs, :], op0=ALU.mult, op1=ALU.max
+                )
+                nc.sync.dma_start(out=out_view[c // 2, c % 2][:, rs, :], in_=y[:, rs, :])
+
+            acc = {}
+            for w, ws, kind in ((wg_sb, wgs, "gamma"), (wb_sb, wbs, "beta")):
+                for r in (2 * half, 2 * half + 1):
+                    ps = psum.tile([P, C], F32, name="gb_ps", bufs=4)
+                    for gg in range(2):
+                        nc.tensor.matmul_mx(
+                            out=ps[:],
+                            lhsT=a_codes[c, r, gg].bitcast(FP8X4),
+                            lhsT_scale=a_scl[c, r, gg],
+                            rhs=w[:, gg, :].bitcast(FP4X4),
+                            rhs_scale=ws[:, gg, :],
+                            start=(gg == 0),
+                            stop=(gg == 1),
+                        )
+                    acc[kind, r] = ps
+            for r in (2 * half, 2 * half + 1):
+                nc.vector.scalar_tensor_tensor(
+                    out=y[:, r, :],
+                    in0=acc["gamma", r][:],
+                    scalar=1.0,
+                    in1=xn[c, half][:, r % 2, :],
+                    op0=ALU.add,
+                    op1=ALU.mult,
+                )
+            for r in (2 * half, 2 * half + 1):
+                nc.vector.tensor_tensor(out=y[:, r, :], in0=acc["beta", r][:], in1=y[:, r, :], op=ALU.add)
+                if c == CHUNKS - 1:
+                    leaky(slice(r, r + 1))
+            if half == 1 and c < CHUNKS - 1:
+                leaky(slice(0, 2))
+                leaky(slice(2, 4))
+
+        prep(0)
+        permute_wm()
+        stats(0)
+        normalise(0, nc.gpsimd, 0)
+        prep(1)
+        stage1(0)
+        prep(2)
+        normalise(0, nc.vector, 1)
+        stats(1)
+        stage1(1)
+        prep(3)
+        stage2(0, 0)
+        normalise(1, nc.gpsimd, 0)
+        stage2(0, 1)
+        normalise(1, nc.vector, 1)
+        stage1(2)
+        stage2(1, 0)
+        normalise(2, nc.gpsimd, 0)
+        stage2(1, 1)
+        normalise(2, nc.vector, 1)
+        stage1(3, 0)
+        stage1(3, 1)
+        stage2(2, 0)
+        normalise(3, nc.gpsimd, 0)
+        stage2(2, 1)
+        normalise(3, nc.vector, 1)
+        stage2(3, 0)
+        stage2(3, 1)

@@ -24,7 +24,13 @@ R = 4
 CHUNKS = 4
 NT = P * R
 EPS = 1e-5
-VECTOR_INTERLEAVES = ((0, None, 0), (3, 1, 1))
+XB = P + 16
+MM_BANKS = 5
+TR_BANKS = 3
+SCALAR_INTERLEAVES = ()
+VECTOR_WIDENS = ((0, 0), (0, 1))
+VECTOR_EMPTIES = ((0, 1),)
+SCALAR_LEAKY = ((2, 0), (2, 1), (2, 2), (2, 3), (3, 0), (3, 1))
 
 
 def tile_spademodulationpointwise_d2p_kernel(
@@ -43,13 +49,15 @@ def tile_spademodulationpointwise_d2p_kernel(
         ms_all = keep.tile([P, 64], F32, name="ms_all")
         nc.scalar.dma_start(out=ms_all[:], in_=m_scale.rearrange("a i j -> (a i j)").partition_broadcast(P))
         m_raw = [keep.tile([P, R, S], U8, name=f"m_raw{c}", align_bytes=64) for c in range(CHUNKS)]
-        x_sb = [keep.tile([P, R, C], BF16, name=f"x_sb{c}", align_bytes=64) for c in range(CHUNKS)]
+        x_sb = [keep.tile([P, R, 4, XB], BF16, name=f"x_sb{c}", align_bytes=64) for c in range(CHUNKS)]
 
         def load_m(c):
             nc.sync.dma_start(out=m_raw[c][:], in_=m_view[c // 2, c % 2])
 
         def load_x(c):
-            nc.sync.dma_start(out=x_sb[c][:], in_=x_view[c // 2, c % 2])
+            nc.sync.dma_start(
+                out=x_sb[c][:, :, :, 0:P], in_=x_view[c // 2, c % 2].rearrange("p r (b c) -> p r b c", c=P)
+            )
 
         wm_raw = keep.tile([P, 2 * K], U8, name="wm_raw", align_bytes=64)
         wms_raw = keep.tile([P, K], U8, name="wms_raw", align_bytes=64)
@@ -64,7 +72,9 @@ def tile_spademodulationpointwise_d2p_kernel(
         nc.gpsimd.memset(wgs[:].rearrange("p g n -> p (g n)").bitcast(I32), 0)
         nc.gpsimd.memset(wbs[:].rearrange("p g n -> p (g n)").bitcast(I32), 0)
 
-        load_m(0)
+        for half in range(2):
+            rs = slice(2 * half, 2 * half + 2)
+            nc.sync.dma_start(out=m_raw[0][:, rs, :], in_=m_view[0, 0][:, rs, :])
         nc.sync.dma_start(out=wm_raw[:], in_=wm_words[0])
         for q in range(4):
             nc.sync.dma_start(
@@ -93,10 +103,10 @@ def tile_spademodulationpointwise_d2p_kernel(
 
         ident = keep.tile([P, P], F32, name="ident")
         make_identity(nc, ident[:])
-        ones_bf = keep.tile([P, P], BF16, name="ones_bf")
-        nc.gpsimd.memset(ones_bf[:], 1.0)
-        ones_f = keep.tile([P, P], F32, name="ones_f")
-        nc.gpsimd.memset(ones_f[:], 1.0)
+        ident_bf = keep.tile([P, P], BF16, name="ident_bf")
+        make_identity(nc, ident_bf[:])
+        for c in range(CHUNKS):
+            nc.gpsimd.memset(x_sb[c][:, :, :, P:XB], 1.0)
 
         sc = keep.tile([P, CHUNKS, 4], F32, name="sc")
         ms_q = ms_all[:].rearrange("p (c q j) -> p c q j", q=4, j=4)
@@ -116,15 +126,15 @@ def tile_spademodulationpointwise_d2p_kernel(
         m_codes = [keep.tile([P, NT], U32, name=f"m_codes{c}", align_bytes=64) for c in range(CHUNKS)]
         m_scl = [keep.tile([P, NT], U8, name=f"m_scl{c}", align_bytes=64) for c in range(CHUNKS)]
 
-        def prep(c):
-            m_bf = work.tile([P, R, S], BF16, name="m_bf", align_bytes=64)
-            m_gr = work.tile([P, R * S], BF16, name="m_gr", align_bytes=64)
-            for half in range(2):
-                rs = slice(2 * half, 2 * half + 2)
-                nc.scalar.copy(
-                    out=m_bf[:, rs, :].rearrange("p r k -> p (r k)"),
-                    in_=m_raw[c][:, rs, :].rearrange("p r k -> p (r k)").bitcast(FP8),
-                )
+        def prep(c, half):
+            m_bf = work.tile([P, 2, S], BF16, name="m_bf", align_bytes=64)
+            m_gr = work.tile([P, 2 * S], BF16, name="m_gr", align_bytes=64)
+            rs = slice(2 * half, 2 * half + 2)
+            widen = nc.vector.tensor_copy if (c, half) in VECTOR_WIDENS else nc.scalar.copy
+            widen(
+                out=m_bf[:].rearrange("p r k -> p (r k)"),
+                in_=m_raw[c][:, rs, :].rearrange("p r k -> p (r k)").bitcast(FP8),
+            )
             for j in range(4):
                 ks = slice(128 * j, 128 * j + 128)
                 nc.vector.tensor_scalar(
@@ -134,17 +144,18 @@ def tile_spademodulationpointwise_d2p_kernel(
                     scalar2=None,
                     op0=ALU.mult,
                 )
-            for half in range(2):
-                tp = psum.tile([P, 2, 2, P], F32, name="tp", bufs=1)
-                for r2 in range(2):
-                    words = m_bf[:, 2 * half + r2, :].bitcast(F32)
-                    for u in range(2):
-                        nc.tensor.transpose(tp[:, r2, u, :], words[:, u : 256 : 2], ident[:])
-                nc.scalar.copy(
-                    out=m_gr[:, 1024 * half : 1024 * half + 1024].bitcast(F32).rearrange("p (r t u) -> p r t u", r=2, u=2),
-                    in_=tp[:].rearrange("p r u t -> p r t u"),
-                )
-            nc.vector.quantize_mx(out=m_codes[c][:].bitcast(FP8X4), scales=m_scl[c][:], in_=m_gr[:])
+            tp = psum.tile([P, 2, 2, P], F32, name="tr_ps", bufs=TR_BANKS)
+            for r in range(2):
+                words = m_bf[:, r, :].bitcast(F32)
+                for u in range(2):
+                    nc.tensor.transpose(tp[:, r, u, :], words[:, u : 256 : 2], ident[:])
+            empty = nc.vector.tensor_copy if (c, half) in VECTOR_EMPTIES else nc.scalar.copy
+            empty(
+                out=m_gr[:].bitcast(F32).rearrange("p (r t u) -> p r t u", r=2, u=2),
+                in_=tp[:].rearrange("p r u t -> p r t u"),
+            )
+            toks = slice(256 * half, 256 * half + 256)
+            nc.vector.quantize_mx(out=m_codes[c][:, toks].bitcast(FP8X4), scales=m_scl[c][:, toks], in_=m_gr[:])
 
         wm_perm = keep.tile([P, 2, 4, 256], U8, name="wm_perm", align_bytes=64)
         wms_perm = keep.tile([P, 2, 4, P], U8, name="wms_perm", align_bytes=64)
@@ -159,47 +170,62 @@ def tile_spademodulationpointwise_d2p_kernel(
                     out=wms_perm[:, gg], in_=wms_raw[:, 512 * gg : 512 * gg + 512].rearrange("p (m t) -> p t m", t=4)
                 )
 
-        nmu = [keep.tile([P, C], F32, name=f"nmu{a}") for a in range(2)]
-        rstd = [keep.tile([P, C], F32, name=f"rstd{a}") for a in range(2)]
+        rstd = [keep.tile([P, 4], F32, name=f"rstd{a}") for a in range(2)]
+        shift = [keep.tile([P, 4], F32, name=f"shift{a}") for a in range(2)]
+        rstd5 = [keep.tile([P, 4], F32, name=f"rstd5{a}") for a in range(2)]
+        shift5 = [keep.tile([P, 4], F32, name=f"shift5{a}") for a in range(2)]
 
         def stats(a):
-            tiles = [x_sb[2 * a + h][:, r, :] for h in range(2) for r in range(R)]
-            s1 = psum.tile([P, C], F32, name="gb_ps", bufs=4)
-            for i, t in enumerate(tiles):
-                nc.tensor.matmul(s1[:], lhsT=ones_bf[:], rhs=t, start=(i == 0), stop=(i == 7))
-            gram = psum.tile([P, 4, P], F32, name="gb_ps", bufs=4)
-            for b in range(4):
-                cols = slice(128 * b, 128 * b + 128)
-                for i, t in enumerate(tiles):
-                    nc.tensor.matmul(gram[:, b, :], lhsT=t[:, cols], rhs=t[:, cols], start=(i == 0), stop=(i == 7))
+            tiles = [x_sb[2 * a + h][:, r] for h in range(2) for r in range(R)]
+            ss = work.tile([P, 4], F32, name="ss")
+            nmean = work.tile([P, 4], F32, name="nmean")
             diag = work.tile([P, 4, P], F32, name="diag")
-            nc.vector.tensor_tensor(
-                out=diag[:], in0=gram[:], in1=ident[:].unsqueeze(1).to_broadcast([P, 4, P]), op=ALU.mult
-            )
-            s2 = psum.tile([P, C], F32, name="gb_ps", bufs=4)
-            nc.tensor.matmul(s2[:], lhsT=ones_f[:], rhs=diag[:].rearrange("p b c -> p (b c)"), start=True, stop=True)
-            musq = work.tile([P, C], F32, name="musq")
-            nc.scalar.activation(out=nmu[a][:], in_=s1[:], func=ACT.Copy, scale=-1.0 / 1024.0)
-            nc.scalar.activation(out=musq[:], in_=s1[:], func=ACT.Square, scale=1.0 / 1024.0)
-            var = work.tile([P, C], F32, name="var")
+            for pair in range(2):
+                gram = psum.tile([P, 2, P + 2], F32, name="mm_ps", bufs=MM_BANKS)
+                for k in range(2):
+                    b = 2 * pair + k
+                    for i, t in enumerate(tiles):
+                        nc.tensor.matmul(
+                            gram[:, k, :], lhsT=t[:, b, 0:P], rhs=t[:, b, 0 : P + 2], start=(i == 0), stop=(i == 7)
+                        )
+                bs = slice(2 * pair, 2 * pair + 2)
+                nc.vector.tensor_tensor(
+                    out=diag[:, bs, :],
+                    in0=gram[:, :, 0:P],
+                    in1=ident[:].unsqueeze(1).to_broadcast([P, 2, P]),
+                    op=ALU.mult,
+                )
+                nc.vector.tensor_scalar(
+                    out=nmean[:, bs], in0=gram[:, :, P], scalar1=-1.0 / 1024.0, scalar2=None, op0=ALU.mult
+                )
+            nc.vector.tensor_reduce(out=ss[:], in_=diag[:], op=ALU.add, axis=mybir.AxisListType.X)
+            msq = work.tile([P, 4], F32, name="msq")
+            nc.vector.tensor_tensor(out=msq[:], in0=nmean[:], in1=nmean[:], op=ALU.mult)
             nc.vector.scalar_tensor_tensor(
-                out=var[:], in0=s2[:], scalar=1.0 / 1024.0, in1=musq[:], op0=ALU.mult, op1=ALU.subtract
+                out=ss[:], in0=ss[:], scalar=1.0 / 1024.0, in1=msq[:], op0=ALU.mult, op1=ALU.subtract
             )
-            nc.scalar.activation(out=rstd[a][:], in_=var[:], func=ACT.Abs_reciprocal_sqrt, bias=EPS)
+            nc.scalar.activation(out=rstd[a][:], in_=ss[:], func=ACT.Abs_reciprocal_sqrt, bias=EPS)
+            nc.gpsimd.tensor_tensor(out=shift[a][:], in0=nmean[:], in1=rstd[a][:], op=ALU.mult)
+            nc.gpsimd.tensor_scalar(out=rstd5[a][:], in0=rstd[a][:], scalar1=0.2, scalar2=0.0, op0=ALU.mult, op1=ALU.add)
+            nc.gpsimd.tensor_scalar(out=shift5[a][:], in0=shift[a][:], scalar1=0.2, scalar2=0.0, op0=ALU.mult, op1=ALU.add)
 
-        xn = {}
+        xn = [keep.tile([P, 4, NT], F32, name=f"xn{c}") for c in range(CHUNKS)]
 
-        def normalise(c, engine, half):
+        def normalise(c, pair):
             a = c // 2
-            rs = slice(2 * half, 2 * half + 2)
-            t = work.tile([P, 2, C], F32, name=f"xn{half}", bufs=1 + half)
-            engine.tensor_tensor(
-                out=t[:], in0=x_sb[c][:, rs, :], in1=nmu[a][:].unsqueeze(1).to_broadcast([P, 2, C]), op=ALU.add
-            )
-            engine.tensor_tensor(
-                out=t[:], in0=t[:], in1=rstd[a][:].unsqueeze(1).to_broadcast([P, 2, C]), op=ALU.mult
-            )
-            xn[c, half] = t
+            xt = psum.tile([P, 2, NT], BF16, name="tr_ps", bufs=TR_BANKS)
+            for k in range(2):
+                for r in range(R):
+                    nc.tensor.transpose(xt[:, k, P * r : P * r + P], x_sb[c][:, r, 2 * pair + k, 0:P], ident_bf[:])
+            for k in range(2):
+                b = 2 * pair + k
+                nc.scalar.activation(
+                    out=xn[c][:, b, :],
+                    in_=xt[:, k, :],
+                    func=ACT.Identity,
+                    bias=(shift5 if (c, b) in SCALAR_LEAKY else shift)[a][:, b : b + 1],
+                    scale=(rstd5 if (c, b) in SCALAR_LEAKY else rstd)[a][:, b : b + 1],
+                )
 
         a_codes = {}
         a_scl = {}
@@ -209,7 +235,7 @@ def tile_spademodulationpointwise_d2p_kernel(
             for gg in range(2):
                 yb = work.tile([P, 4, n], BF16, name="yb", align_bytes=64)
                 for t in range(4):
-                    h = psum.tile([P, n], F32, name="h_ps", bufs=3)
+                    h = psum.tile([P, n], F32, name="mm_ps", bufs=MM_BANKS)
                     nc.tensor.matmul_mx(
                         out=h[:],
                         lhsT=wm_perm[:, gg, t, :].bitcast(FP4X4),
@@ -232,88 +258,101 @@ def tile_spademodulationpointwise_d2p_kernel(
                     )
                 ag = work.tile([P, n, 4], BF16, name="ag", align_bytes=64)
                 ysrc = yb[:].rearrange("p t n -> p n t")
-                if (c, half, gg) in VECTOR_INTERLEAVES:
+                if (c, half, gg) not in SCALAR_INTERLEAVES:
                     nc.vector.tensor_copy(out=ag[:], in_=ysrc)
                 else:
                     nc.scalar.copy(out=ag[:], in_=ysrc)
-                codes = work.tile([P, n], U32, name=f"a_codes{gg}", align_bytes=64)
-                scl = work.tile([P, n], U8, name=f"a_scl{gg}", align_bytes=64)
-                nc.vector.quantize_mx(out=codes[:].bitcast(FP8X4), scales=scl[:], in_=ag[:].rearrange("p n t -> p (n t)"))
-                for r in range(lo // P, (lo + n) // P):
-                    toks = slice(P * r - lo, P * r - lo + P)
-                    a_codes[c, r, gg] = codes[:, toks]
-                    a_scl[c, r, gg] = scl[:, toks]
-
-        y_tiles = {}
-
-        def stage2(c, half):
-            if half == 0:
-                y_tiles[c] = work.tile([P, R, C], F32, name="y")
-            y = y_tiles[c]
-
-            def leaky(rs):
-                nc.vector.scalar_tensor_tensor(
-                    out=y[:, rs, :], in0=y[:, rs, :], scalar=0.2, in1=y[:, rs, :], op0=ALU.mult, op1=ALU.max
+                if lo == 0:
+                    a_codes[c, gg] = work.tile([P, NT], U32, name=f"a_codes{gg}", align_bytes=64)
+                    a_scl[c, gg] = work.tile([P, NT], U8, name=f"a_scl{gg}", align_bytes=64)
+                nc.vector.quantize_mx(
+                    out=a_codes[c, gg][:, lo : lo + n].bitcast(FP8X4),
+                    scales=a_scl[c, gg][:, lo : lo + n],
+                    in_=ag[:].rearrange("p n t -> p (n t)"),
                 )
-                nc.sync.dma_start(out=out_view[c // 2, c % 2][:, rs, :], in_=y[:, rs, :])
 
-            acc = {}
-            for w, ws, kind in ((wg_sb, wgs, "gamma"), (wb_sb, wbs, "beta")):
-                for r in (2 * half, 2 * half + 1):
-                    ps = psum.tile([P, C], F32, name="gb_ps", bufs=4)
-                    for gg in range(2):
-                        nc.tensor.matmul_mx(
-                            out=ps[:],
-                            lhsT=a_codes[c, r, gg].bitcast(FP8X4),
-                            lhsT_scale=a_scl[c, r, gg],
-                            rhs=w[:, gg, :].bitcast(FP4X4),
-                            rhs_scale=ws[:, gg, :],
-                            start=(gg == 0),
-                            stop=(gg == 1),
-                        )
-                    acc[kind, r] = ps
-            for r in (2 * half, 2 * half + 1):
+        o_tiles = {}
+
+        def stage2(c, b):
+            if b == 0:
+                o_tiles[c] = work.tile([P, R, C], F32, name="o")
+            o = o_tiles[c]
+            acc = []
+            for w, ws in ((wg_sb, wgs), (wb_sb, wbs)):
+                ps = psum.tile([P, NT], F32, name="mm_ps", bufs=MM_BANKS)
+                for gg in range(2):
+                    nc.tensor.matmul_mx(
+                        out=ps[:],
+                        lhsT=w[:, gg, 256 * b : 256 * b + 256].bitcast(FP4X4),
+                        lhsT_scale=ws[:, gg, P * b : P * b + P],
+                        rhs=a_codes[c, gg][:].bitcast(FP8X4),
+                        rhs_scale=a_scl[c, gg][:],
+                        start=(gg == 0),
+                        stop=(gg == 1),
+                    )
+                acc.append(ps)
+            y = work.tile([P, NT], F32, name="y", bufs=3)
+            nc.vector.scalar_tensor_tensor(
+                out=y[:], in0=acc[0][:], scalar=1.0, in1=xn[c][:, b, :], op0=ALU.add, op1=ALU.mult
+            )
+            ot = psum.tile([P, R, P], F32, name="tr_ps", bufs=TR_BANKS)
+            if (c, b) in SCALAR_LEAKY:
                 nc.vector.scalar_tensor_tensor(
-                    out=y[:, r, :],
-                    in0=acc["gamma", r][:],
-                    scalar=1.0,
-                    in1=xn[c, half][:, r % 2, :],
-                    op0=ALU.add,
-                    op1=ALU.mult,
+                    out=y[:], in0=acc[1][:], scalar=0.2, in1=y[:], op0=ALU.mult, op1=ALU.add
                 )
-            for r in (2 * half, 2 * half + 1):
-                nc.vector.tensor_tensor(out=y[:, r, :], in0=acc["beta", r][:], in1=y[:, r, :], op=ALU.add)
-                if c == CHUNKS - 1:
-                    leaky(slice(r, r + 1))
-            if half == 1 and c < CHUNKS - 1:
-                leaky(slice(0, 2))
-                leaky(slice(2, 4))
+                pos = work.tile([P, NT], F32, name="pos")
+                nc.scalar.activation(out=pos[:], in_=y[:], func=ACT.Relu, scale=4.0)
+                for r in range(R):
+                    toks = slice(P * r, P * r + P)
+                    nc.tensor.matmul(
+                        ot[:, r, :], lhsT=y[:, toks], rhs=ident[:], is_transpose=True, start=True, stop=False
+                    )
+                    nc.tensor.matmul(
+                        ot[:, r, :], lhsT=pos[:, toks], rhs=ident[:], is_transpose=True, start=False, stop=True
+                    )
+            else:
+                nc.vector.tensor_tensor(out=y[:], in0=acc[1][:], in1=y[:], op=ALU.add)
+                nc.vector.scalar_tensor_tensor(out=y[:], in0=y[:], scalar=0.2, in1=y[:], op0=ALU.mult, op1=ALU.max)
+                for r in range(R):
+                    nc.tensor.transpose(ot[:, r, :], y[:, P * r : P * r + P], ident[:])
+            nc.scalar.copy(out=o[:, :, P * b : P * b + P], in_=ot[:])
+            if c == CHUNKS - 1:
+                cols = slice(P * b, P * b + P)
+                nc.sync.dma_start(out=out_view[c // 2, c % 2][:, :, cols], in_=o[:, :, cols])
+            elif b % 2 == 1:
+                cols = slice(P * (b - 1), P * (b + 1))
+                nc.sync.dma_start(out=out_view[c // 2, c % 2][:, :, cols], in_=o[:, :, cols])
 
-        prep(0)
+        prep(0, 0)
         permute_wm()
+        prep(0, 1)
+        stage1(0, 0)
+        stage1(0, 1)
+        prep(1, 0)
+        prep(1, 1)
         stats(0)
-        normalise(0, nc.gpsimd, 0)
-        prep(1)
-        stage1(0)
-        prep(2)
-        normalise(0, nc.vector, 1)
-        stats(1)
         stage1(1)
-        prep(3)
-        stage2(0, 0)
-        normalise(1, nc.gpsimd, 0)
-        stage2(0, 1)
-        normalise(1, nc.vector, 1)
+        prep(2, 0)
+        prep(2, 1)
+        normalise(0, 0)
+        normalise(0, 1)
+        stats(1)
+        for b in range(4):
+            stage2(0, b)
         stage1(2)
-        stage2(1, 0)
-        normalise(2, nc.gpsimd, 0)
-        stage2(1, 1)
-        normalise(2, nc.vector, 1)
+        prep(3, 0)
+        prep(3, 1)
+        normalise(1, 0)
+        normalise(1, 1)
+        for b in range(4):
+            stage2(1, b)
         stage1(3, 0)
         stage1(3, 1)
-        stage2(2, 0)
-        normalise(3, nc.gpsimd, 0)
-        stage2(2, 1)
-        normalise(3, nc.vector, 1)
-        stage2(3, 0)
-        stage2(3, 1)
+        normalise(2, 0)
+        normalise(2, 1)
+        for b in range(4):
+            stage2(2, b)
+        normalise(3, 0)
+        normalise(3, 1)
+        for b in range(4):
+            stage2(3, b)

from contextlib import ExitStack

import concourse.mybir as mybir
from concourse.masks import make_identity

F32 = mybir.dt.float32
BF16 = mybir.dt.bfloat16
U32 = mybir.dt.uint32
I32 = mybir.dt.int32
U8 = mybir.dt.uint8
FP8 = mybir.dt.float8_e4m3fn
FP8X4 = mybir.dt.float8_e4m3fn_x4
FP4X4 = mybir.dt.float4_e2m1fn_x4
ALU = mybir.AluOpType
ACT = mybir.ActivationFunctionType

FLOPS = 2 * 2048 * 512 * 1024 + 2 * 2 * 2048 * 1024 * 512

P = 128
S = 512
K = 1024
C = 512
R = 4
CHUNKS = 4
NT = P * R
EPS = 1e-5
XB = P + 16
MM_BANKS = 5
TR_BANKS = 3
SCALAR_INTERLEAVES = ()
VECTOR_WIDENS = ((0, 0), (0, 1))
VECTOR_EMPTIES = ((0, 1),)
SCALAR_LEAKY = ((2, 0), (2, 1), (2, 2), (2, 3), (3, 0), (3, 1))


def tile_spademodulationpointwise_d2p_kernel(
    tc, x, m_bytes, m_scale, wm_words, wm_scales, bm, g, wg_words, wg_scales, wb_words, wb_scales, out
):
    nc = tc.nc
    m_view = m_bytes.rearrange("a (h p r) k -> a h p r k", h=2, p=P, r=R)
    x_view = x.rearrange("a (h p r) c -> a h p r c", h=2, p=P, r=R)
    out_view = out.rearrange("a (h p r) c -> a h p r c", h=2, p=P, r=R)

    with ExitStack() as ctx:
        keep = ctx.enter_context(tc.tile_pool(name="keep", bufs=1))
        work = ctx.enter_context(tc.tile_pool(name="work", bufs=2))
        psum = ctx.enter_context(tc.psum_pool(name="psum", bufs=1))

        ms_all = keep.tile([P, 64], F32, name="ms_all")
        nc.scalar.dma_start(out=ms_all[:], in_=m_scale.rearrange("a i j -> (a i j)").partition_broadcast(P))
        m_raw = [keep.tile([P, R, S], U8, name=f"m_raw{c}", align_bytes=64) for c in range(CHUNKS)]
        x_sb = [keep.tile([P, R, 4, XB], BF16, name=f"x_sb{c}", align_bytes=64) for c in range(CHUNKS)]

        def load_m(c):
            nc.sync.dma_start(out=m_raw[c][:], in_=m_view[c // 2, c % 2])

        def load_x(c):
            nc.sync.dma_start(
                out=x_sb[c][:, :, :, 0:P], in_=x_view[c // 2, c % 2].rearrange("p r (b c) -> p r b c", c=P)
            )

        wm_raw = keep.tile([P, 2 * K], U8, name="wm_raw", align_bytes=64)
        wms_raw = keep.tile([P, K], U8, name="wms_raw", align_bytes=64)
        wg_sb = keep.tile([P, 2, 2 * C], U8, name="wg_sb", align_bytes=64)
        wb_sb = keep.tile([P, 2, 2 * C], U8, name="wb_sb", align_bytes=64)
        wgs = keep.tile([P, 2, C], U8, name="wgs", align_bytes=64)
        wbs = keep.tile([P, 2, C], U8, name="wbs", align_bytes=64)
        g_bf = keep.tile([P, 2, 4], BF16, name="g_bf")
        bm_bf = keep.tile([P, 2, 4], BF16, name="bm_bf")

        nc.gpsimd.memset(wms_raw[:].bitcast(I32), 0)
        nc.gpsimd.memset(wgs[:].rearrange("p g n -> p (g n)").bitcast(I32), 0)
        nc.gpsimd.memset(wbs[:].rearrange("p g n -> p (g n)").bitcast(I32), 0)

        for half in range(2):
            rs = slice(2 * half, 2 * half + 2)
            nc.sync.dma_start(out=m_raw[0][:, rs, :], in_=m_view[0, 0][:, rs, :])
        nc.sync.dma_start(out=wm_raw[:], in_=wm_words[0])
        for q in range(4):
            nc.sync.dma_start(
                out=wms_raw[32 * q : 32 * q + 4, :].bitcast(I32), in_=wm_scales[0, 4 * q : 4 * q + 4, :].bitcast(I32)
            )
        nc.scalar.dma_start(out=g_bf[:], in_=g.rearrange("(g p t) -> p g t", p=P, t=4))
        nc.scalar.dma_start(out=bm_bf[:], in_=bm.rearrange("(g p t) -> p g t", p=P, t=4))
        load_x(0)
        load_x(1)
        load_m(1)
        for q in range(4):
            nc.sync.dma_start(
                out=wgs[32 * q : 32 * q + 4].bitcast(I32),
                in_=wg_scales[:, 4 * q : 4 * q + 4, :].rearrange("g q n -> q g n").bitcast(I32),
            )
            nc.sync.dma_start(
                out=wbs[32 * q : 32 * q + 4].bitcast(I32),
                in_=wb_scales[:, 4 * q : 4 * q + 4, :].rearrange("g q n -> q g n").bitcast(I32),
            )
        nc.sync.dma_start(out=wg_sb[:], in_=wg_words.rearrange("g p n -> p g n"))
        nc.sync.dma_start(out=wb_sb[:], in_=wb_words.rearrange("g p n -> p g n"))
        load_m(2)
        load_m(3)
        load_x(2)
        load_x(3)

        ident = keep.tile([P, P], F32, name="ident")
        make_identity(nc, ident[:])
        ident_bf = keep.tile([P, P], BF16, name="ident_bf")
        make_identity(nc, ident_bf[:])
        for c in range(CHUNKS):
            nc.gpsimd.memset(x_sb[c][:, :, :, P:XB], 1.0)

        sc = keep.tile([P, CHUNKS, 4], F32, name="sc")
        ms_q = ms_all[:].rearrange("p (c q j) -> p c q j", q=4, j=4)
        for q in range(4):
            rows = slice(32 * q, 32 * q + 32)
            nc.gpsimd.tensor_copy(out=sc[rows], in_=ms_q[rows, :, q, :])

        sg = keep.tile([P, 8], F32, name="sg")
        ga = keep.tile([P, 8], F32, name="ga")
        gb = keep.tile([P, 8], F32, name="gb")
        g_flat = g_bf[:].rearrange("p g t -> p (g t)")
        nc.vector.tensor_scalar(out=sg[:], in0=g_flat, scalar1=0.0, scalar2=2.0, op0=ALU.is_ge, op1=ALU.mult)
        nc.vector.tensor_scalar(out=sg[:], in0=sg[:], scalar1=-1.0, scalar2=None, op0=ALU.add)
        nc.vector.tensor_tensor(out=ga[:], in0=g_flat, in1=sg[:], op=ALU.mult)
        nc.vector.tensor_tensor(out=gb[:], in0=bm_bf[:].rearrange("p g t -> p (g t)"), in1=ga[:], op=ALU.mult)

        m_codes = [keep.tile([P, NT], U32, name=f"m_codes{c}", align_bytes=64) for c in range(CHUNKS)]
        m_scl = [keep.tile([P, NT], U8, name=f"m_scl{c}", align_bytes=64) for c in range(CHUNKS)]

        def prep(c, half):
            m_bf = work.tile([P, 2, S], BF16, name="m_bf", align_bytes=64)
            m_gr = work.tile([P, 2 * S], BF16, name="m_gr", align_bytes=64)
            rs = slice(2 * half, 2 * half + 2)
            widen = nc.vector.tensor_copy if (c, half) in VECTOR_WIDENS else nc.scalar.copy
            widen(
                out=m_bf[:].rearrange("p r k -> p (r k)"),
                in_=m_raw[c][:, rs, :].rearrange("p r k -> p (r k)").bitcast(FP8),
            )
            for j in range(4):
                ks = slice(128 * j, 128 * j + 128)
                nc.vector.tensor_scalar(
                    out=m_bf[:, :, ks],
                    in0=m_bf[:, :, ks],
                    scalar1=sc[:, c, j : j + 1],
                    scalar2=None,
                    op0=ALU.mult,
                )
            tp = psum.tile([P, 2, 2, P], F32, name="tr_ps", bufs=TR_BANKS)
            for r in range(2):
                words = m_bf[:, r, :].bitcast(F32)
                for u in range(2):
                    nc.tensor.transpose(tp[:, r, u, :], words[:, u : 256 : 2], ident[:])
            empty = nc.vector.tensor_copy if (c, half) in VECTOR_EMPTIES else nc.scalar.copy
            empty(
                out=m_gr[:].bitcast(F32).rearrange("p (r t u) -> p r t u", r=2, u=2),
                in_=tp[:].rearrange("p r u t -> p r t u"),
            )
            toks = slice(256 * half, 256 * half + 256)
            nc.vector.quantize_mx(out=m_codes[c][:, toks].bitcast(FP8X4), scales=m_scl[c][:, toks], in_=m_gr[:])

        wm_perm = keep.tile([P, 2, 4, 256], U8, name="wm_perm", align_bytes=64)
        wms_perm = keep.tile([P, 2, 4, P], U8, name="wms_perm", align_bytes=64)

        def permute_wm():
            for gg in range(2):
                nc.vector.tensor_copy(
                    out=wm_perm[:, gg].rearrange("p t (m b) -> p t m b", b=2),
                    in_=wm_raw[:, 1024 * gg : 1024 * gg + 1024].rearrange("p (m t b) -> p t m b", t=4, b=2),
                )
                nc.vector.tensor_copy(
                    out=wms_perm[:, gg], in_=wms_raw[:, 512 * gg : 512 * gg + 512].rearrange("p (m t) -> p t m", t=4)
                )

        rstd = [keep.tile([P, 4], F32, name=f"rstd{a}") for a in range(2)]
        shift = [keep.tile([P, 4], F32, name=f"shift{a}") for a in range(2)]
        rstd5 = [keep.tile([P, 4], F32, name=f"rstd5{a}") for a in range(2)]
        shift5 = [keep.tile([P, 4], F32, name=f"shift5{a}") for a in range(2)]

        def stats(a):
            tiles = [x_sb[2 * a + h][:, r] for h in range(2) for r in range(R)]
            ss = work.tile([P, 4], F32, name="ss")
            nmean = work.tile([P, 4], F32, name="nmean")
            diag = work.tile([P, 4, P], F32, name="diag")
            for pair in range(2):
                gram = psum.tile([P, 2, P + 2], F32, name="mm_ps", bufs=MM_BANKS)
                for k in range(2):
                    b = 2 * pair + k
                    for i, t in enumerate(tiles):
                        nc.tensor.matmul(
                            gram[:, k, :], lhsT=t[:, b, 0:P], rhs=t[:, b, 0 : P + 2], start=(i == 0), stop=(i == 7)
                        )
                bs = slice(2 * pair, 2 * pair + 2)
                nc.vector.tensor_tensor(
                    out=diag[:, bs, :],
                    in0=gram[:, :, 0:P],
                    in1=ident[:].unsqueeze(1).to_broadcast([P, 2, P]),
                    op=ALU.mult,
                )
                nc.vector.tensor_scalar(
                    out=nmean[:, bs], in0=gram[:, :, P], scalar1=-1.0 / 1024.0, scalar2=None, op0=ALU.mult
                )
            nc.vector.tensor_reduce(out=ss[:], in_=diag[:], op=ALU.add, axis=mybir.AxisListType.X)
            msq = work.tile([P, 4], F32, name="msq")
            nc.vector.tensor_tensor(out=msq[:], in0=nmean[:], in1=nmean[:], op=ALU.mult)
            nc.vector.scalar_tensor_tensor(
                out=ss[:], in0=ss[:], scalar=1.0 / 1024.0, in1=msq[:], op0=ALU.mult, op1=ALU.subtract
            )
            nc.scalar.activation(out=rstd[a][:], in_=ss[:], func=ACT.Abs_reciprocal_sqrt, bias=EPS)
            nc.gpsimd.tensor_tensor(out=shift[a][:], in0=nmean[:], in1=rstd[a][:], op=ALU.mult)
            nc.gpsimd.tensor_scalar(out=rstd5[a][:], in0=rstd[a][:], scalar1=0.2, scalar2=0.0, op0=ALU.mult, op1=ALU.add)
            nc.gpsimd.tensor_scalar(out=shift5[a][:], in0=shift[a][:], scalar1=0.2, scalar2=0.0, op0=ALU.mult, op1=ALU.add)

        xn = [keep.tile([P, 4, NT], F32, name=f"xn{c}") for c in range(CHUNKS)]

        def normalise(c, pair):
            a = c // 2
            xt = psum.tile([P, 2, NT], BF16, name="tr_ps", bufs=TR_BANKS)
            for k in range(2):
                for r in range(R):
                    nc.tensor.transpose(xt[:, k, P * r : P * r + P], x_sb[c][:, r, 2 * pair + k, 0:P], ident_bf[:])
            for k in range(2):
                b = 2 * pair + k
                nc.scalar.activation(
                    out=xn[c][:, b, :],
                    in_=xt[:, k, :],
                    func=ACT.Identity,
                    bias=(shift5 if (c, b) in SCALAR_LEAKY else shift)[a][:, b : b + 1],
                    scale=(rstd5 if (c, b) in SCALAR_LEAKY else rstd)[a][:, b : b + 1],
                )

        a_codes = {}
        a_scl = {}

        def stage1(c, half=None):
            lo, n = (0, NT) if half is None else (half * NT // 2, NT // 2)
            for gg in range(2):
                yb = work.tile([P, 4, n], BF16, name="yb", align_bytes=64)
                for t in range(4):
                    h = psum.tile([P, n], F32, name="mm_ps", bufs=MM_BANKS)
                    nc.tensor.matmul_mx(
                        out=h[:],
                        lhsT=wm_perm[:, gg, t, :].bitcast(FP4X4),
                        lhsT_scale=wms_perm[:, gg, t, :],
                        rhs=m_codes[c][:, lo : lo + n].bitcast(FP8X4),
                        rhs_scale=m_scl[c][:, lo : lo + n],
                        start=True,
                        stop=True,
                    )
                    col = 4 * gg + t
                    nc.scalar.activation(
                        out=yb[:, t, :],
                        in_=h[:],
                        func=ACT.Relu,
                        bias=gb[:, col : col + 1],
                        scale=ga[:, col : col + 1],
                    )
                    nc.vector.tensor_scalar(
                        out=yb[:, t, :], in0=yb[:, t, :], scalar1=sg[:, col : col + 1], scalar2=None, op0=ALU.mult
                    )
                ag = work.tile([P, n, 4], BF16, name="ag", align_bytes=64)
                ysrc = yb[:].rearrange("p t n -> p n t")
                if (c, half, gg) not in SCALAR_INTERLEAVES:
                    nc.vector.tensor_copy(out=ag[:], in_=ysrc)
                else:
                    nc.scalar.copy(out=ag[:], in_=ysrc)
                if lo == 0:
                    a_codes[c, gg] = work.tile([P, NT], U32, name=f"a_codes{gg}", align_bytes=64)
                    a_scl[c, gg] = work.tile([P, NT], U8, name=f"a_scl{gg}", align_bytes=64)
                nc.vector.quantize_mx(
                    out=a_codes[c, gg][:, lo : lo + n].bitcast(FP8X4),
                    scales=a_scl[c, gg][:, lo : lo + n],
                    in_=ag[:].rearrange("p n t -> p (n t)"),
                )

        o_tiles = {}

        def stage2(c, b):
            if b == 0:
                o_tiles[c] = work.tile([P, R, C], F32, name="o")
            o = o_tiles[c]
            acc = []
            for w, ws in ((wg_sb, wgs), (wb_sb, wbs)):
                ps = psum.tile([P, NT], F32, name="mm_ps", bufs=MM_BANKS)
                for gg in range(2):
                    nc.tensor.matmul_mx(
                        out=ps[:],
                        lhsT=w[:, gg, 256 * b : 256 * b + 256].bitcast(FP4X4),
                        lhsT_scale=ws[:, gg, P * b : P * b + P],
                        rhs=a_codes[c, gg][:].bitcast(FP8X4),
                        rhs_scale=a_scl[c, gg][:],
                        start=(gg == 0),
                        stop=(gg == 1),
                    )
                acc.append(ps)
            y = work.tile([P, NT], F32, name="y", bufs=3)
            nc.vector.scalar_tensor_tensor(
                out=y[:], in0=acc[0][:], scalar=1.0, in1=xn[c][:, b, :], op0=ALU.add, op1=ALU.mult
            )
            ot = psum.tile([P, R, P], F32, name="tr_ps", bufs=TR_BANKS)
            if (c, b) in SCALAR_LEAKY:
                nc.vector.scalar_tensor_tensor(
                    out=y[:], in0=acc[1][:], scalar=0.2, in1=y[:], op0=ALU.mult, op1=ALU.add
                )
                pos = work.tile([P, NT], F32, name="pos")
                nc.scalar.activation(out=pos[:], in_=y[:], func=ACT.Relu, scale=4.0)
                for r in range(R):
                    toks = slice(P * r, P * r + P)
                    nc.tensor.matmul(
                        ot[:, r, :], lhsT=y[:, toks], rhs=ident[:], is_transpose=True, start=True, stop=False
                    )
                    nc.tensor.matmul(
                        ot[:, r, :], lhsT=pos[:, toks], rhs=ident[:], is_transpose=True, start=False, stop=True
                    )
            else:
                nc.vector.tensor_tensor(out=y[:], in0=acc[1][:], in1=y[:], op=ALU.add)
                nc.vector.scalar_tensor_tensor(out=y[:], in0=y[:], scalar=0.2, in1=y[:], op0=ALU.mult, op1=ALU.max)
                for r in range(R):
                    nc.tensor.transpose(ot[:, r, :], y[:, P * r : P * r + P], ident[:])
            nc.scalar.copy(out=o[:, :, P * b : P * b + P], in_=ot[:])
            if c == CHUNKS - 1:
                cols = slice(P * b, P * b + P)
                nc.sync.dma_start(out=out_view[c // 2, c % 2][:, :, cols], in_=o[:, :, cols])
            elif b % 2 == 1:
                cols = slice(P * (b - 1), P * (b + 1))
                nc.sync.dma_start(out=out_view[c // 2, c % 2][:, :, cols], in_=o[:, :, cols])

        prep(0, 0)
        permute_wm()
        prep(0, 1)
        stage1(0, 0)
        stage1(0, 1)
        prep(1, 0)
        prep(1, 1)
        stats(0)
        stage1(1)
        prep(2, 0)
        prep(2, 1)
        normalise(0, 0)
        normalise(0, 1)
        stats(1)
        for b in range(4):
            stage2(0, b)
        stage1(2)
        prep(3, 0)
        prep(3, 1)
        normalise(1, 0)
        normalise(1, 1)
        for b in range(4):
            stage2(1, b)
        stage1(3, 0)
        stage1(3, 1)
        normalise(2, 0)
        normalise(2, 1)
        for b in range(4):
            stage2(2, b)
        normalise(3, 0)
        normalise(3, 1)
        for b in range(4):
            stage2(3, b)
